import numpy as np, ml_dtypes
CORES = [13,21,141,149]
N = 4
import mx_ref
NC = 128
def at(b): return (b, 0) if b < N else (2 * N - 1 - b, 1)
BF = ml_dtypes.bfloat16
def setup_inputs(rng):
    def f(*shape):
        return mx_ref.flush((rng.standard_normal(shape, dtype=np.float32) * np.exp2(rng.integers(-2, 3, shape[:-1] + (1,)))).astype(BF))
    return {"k": f(N, 128, 2 * 512), "q": f(N, 128, 2 * 4 * NC)}
def setup_inputs_blocks(rng):
    d = setup_inputs(rng)
    for k in ("k", "q"): d[k] = mx_ref.spread(d[k], rng, 4)
    return d
def setup_inputs_wide(rng):
    d = setup_inputs(rng)
    for k in ("k", "q"): d[k] = mx_ref.flush((d[k].astype(np.float32) * np.exp2(rng.integers(-8, 9, (N, 1, 1))).astype(np.float32)).astype(BF))
    return d
def setup_inputs_zeros(rng):
    d = setup_inputs(rng); v = d["q"].reshape(N, 128, -1, 4).copy()
    v[np.broadcast_to((rng.random((N, 1, v.shape[2], 1)) < 0.33), v.shape)] = 0
    d["q"] = v.reshape(d["q"].shape)
    return d
def reference(k, q):
    QK = [mx_ref.quantize(k[at(b)[0]][:, 512 * at(b)[1]:512 * at(b)[1] + 512]) for b in range(2 * N)]
    QQ = [mx_ref.quantize(q[at(b)[0]][:, 4 * NC * at(b)[1]:4 * NC * at(b)[1] + 4 * NC]) for b in range(2 * N)]
    y = np.zeros((N, 128, (2 * N + 1) * NC), np.float32)
    for r in range(N):
        c = 0
        for a in (r, 2 * N - 1 - r):
            for b in range(a + 1):
                y[r][:, c:c + NC] = mx_ref.matmul(QK[b], QQ[a]); c += NC
    return {"y": y}

from concourse.bass import DstId, RemoteDMATransfer
from concourse.mybir import dt, ActivationFunctionType

N = 4
NB = 2 * N
W = 128
E = 4 * W
BANK = 512
NBANKS = 8
WORLD = 256

SCRATCH = {
    "kb": ("sbuf", [128, 2 * E], "bfloat16"),
    "qb": ("sbuf", [128, 2 * E], "bfloat16"),
    "kc": ("sbuf", [128, NB * W], "float8_e4m3fn_x4"),
    "ks": ("sbuf", [128, NB * W], "uint8"),
    "qc": ("sbuf", [128, 2 * W], "float8_e4m3fn_x4"),
    "qs": ("sbuf", [128, 2 * W], "uint8"),
    "ps": ("psum", [128, NBANKS * BANK], "float32"),
    "yb": ("sbuf", [128, (NB + 1) * W], "float32"),
}
SEMAPHORES = (["kl", "kl2", "ql", "kq", "kq2", "qq", "feed", "fed", "sent", "sty", "sta"]
              + ["in%d" % s for s in range(N)]
              + ["mm%d" % i for i in range(NB + 1)] + ["cp%d" % i for i in range(NB + 1)])


def _block(s, t):
    return s if t == 0 else NB - 1 - s


def _ntiles(s, d):
    return len([t for t in (0, 1) if _block(s, t) <= NB - 1 - d])


def _bits(mask):
    return [1 << i for i in range(mask.bit_length()) if (mask >> i) & 1]


def _split(bits, n):
    k = len(bits) // n
    return [bits[i * k:(i + 1) * k] for i in range(n)]


def _plan(cores, topo):
    direct = dict((s, []) for s in range(N))
    cross = []
    for s in range(N):
        for d in range(N):
            if d != s and _ntiles(s, d):
                if topo.may_write(cores[s], cores[d]):
                    direct[s].append(d)
                else:
                    cross.append((s, d))
    cross.sort(key=lambda f: (-_ntiles(f[0], f[1]), f))
    out, inn, route = {}, {}, {}
    for s, d in cross:
        c = cores[s]
        able = [x for x in range(WORLD) if x != c and topo.host(x) == topo.host(c) and topo.chip(x) == topo.chip(c)
                and topo.may_write(x, cores[d])]
        dies = sorted(set(topo.die(x) for x in able),
                      key=lambda v: (out.get((s, v), 0) + inn.get((d, v), 0), v != topo.die(c)))
        die = dies[0]
        out[(s, die)] = out.get((s, die), 0) + _ntiles(s, d)
        inn[(d, die)] = inn.get((d, die), 0) + _ntiles(s, d)
        pair = [x for x in able if topo.die(x) == die]
        route[(s, d)] = (die, pair[0], pair[1])
    return direct, route


def _feeds(s, kind, cores, route, topo):
    flows = sorted(d for (a, d) in route if a == s)
    same = len(set(_ntiles(s, d) for d in flows)) == 1
    res = []
    for i, d in enumerate(flows):
        relay = route[(s, d)][1 + kind]
        mine = _bits(topo.mask(cores[s], relay))[i::len(flows)]
        n = _ntiles(s, d)
        pieces = [(0, n)] if same else [(t, t + 1) for t in range(n)]
        for j, (a, b) in enumerate(pieces):
            res.append((relay, (2 * s + a) * W, (2 * s + b) * W, sum(_split(mine, len(pieces))[j])))
    return res


def rank_program(g, core, T, topo):
    cores = list(T.cores)
    direct, route = _plan(cores, topo)
    sem = T.sem

    def view(kind, a, b):
        return T.kc[:, a:b].bitcast(dt.uint8) if kind == 0 else T.ks[:, a:b]

    for (s, d), way in route.items():
        for kind in (0, 1):
            if way[1 + kind] == core:
                got = sum(len(_bits(m)) for (x, a, b, m) in _feeds(s, kind, cores, route, topo) if x == core)
                a, b = 2 * s * W, (2 * s + _ntiles(s, d)) * W
                rid, pid = topo.addr(cores[d], core)
                m = topo.mask(core, cores[d])
                g.wait_ge(sem.feed, got)
                g.remote_dma(view(kind, a, b), view(kind, a, b), sem["in%d" % s], sem.sent, pid, rid, m)
                g.wait_ge(sem.sent, len(_bits(m)))

    r = T.rank_of(core)
    if r is None:
        return
    v, te, sc, sy = g.vector, g.tensor, g.scalar, g.sync
    slot = 2 * r * W
    first = max(_ntiles(r, d) for d in range(N) if d != r)

    sy.dma_start(T.kb[:, 0:first * E], T.k[:, 0:first * E]).then_inc(sem.kl, 16)
    if first < 2:
        sy.wait_ge(sem.kl, 16)
        sy.dma_start(T.kb[:, first * E:2 * E], T.k[:, first * E:2 * E]).then_inc(sem.kl2, 16)
    sc.wait_ge(sem.kl, 16)
    sc.dma_start(T.qb[:], T.q[:]).then_inc(sem.ql, 16)

    v.wait_ge(sem.kl, 16)
    v.quantize_mx(T.kc[:, slot:slot + first * W], T.ks[:, slot:slot + first * W], T.kb[:, 0:first * E]).then_inc(sem.kq, 1)
    v.wait_ge(sem.ql, 16)
    v.quantize_mx(T.qc[:], T.qs[:], T.qb[:]).then_inc(sem.qq, 1)
    if first < 2:
        v.wait_ge(sem.kl2, 16)
        v.quantize_mx(T.kc[:, slot + first * W:slot + 2 * W], T.ks[:, slot + first * W:slot + 2 * W],
                      T.kb[:, first * E:2 * E]).then_inc(sem.kq2, 1)

    g.wait_ge(sem.kq, 1)
    fed = 0
    for kind in (0, 1):
        trs = []
        for relay, a, b, m in _feeds(r, kind, cores, route, topo):
            rid, pid = topo.addr(relay, core)
            trs.append(RemoteDMATransfer(dst_ids=[DstId(rid=rid, pnc=pid)], dma_engine_mask=m, remote_sem=sem.feed,
                                         src=view(kind, a, b), dst=view(kind, a, b)))
            fed += len(_bits(m))
        g.remote_dma_fused(trs, local_sem=sem.fed)
    sent = 0
    for d in direct[r]:
        rid, pid = topo.addr(cores[d], core)
        m = topo.mask(core, cores[d])
        a, b = slot, slot + _ntiles(r, d) * W
        for kind in (0, 1):
            g.remote_dma(view(kind, a, b), view(kind, a, b), sem["in%d" % r], sem.sent, pid, rid, m)
            sent += len(_bits(m))
    g.wait_ge(sem.sent, sent)

    relayed = sorted((s for s in range(N) if (s, r) in route),
                     key=lambda s: (_ntiles(s, r), route[(s, r)][0] != topo.die(core), s))
    order = [r] + [s for s in range(N) if r in direct[s]] + relayed
    i = 0
    stores = [0, 0]
    for s in order:
        if s == r:
            te.wait_ge(sem.kq, 1)
            te.wait_ge(sem.qq, 1)
        else:
            senders = [cores[s], cores[s]] if r in direct[s] else list(route[(s, r)][1:])
            te.wait_ge(sem["in%d" % s], sum(len(_bits(topo.mask(x, core))) for x in senders))
        for t in range(2 if s == r else _ntiles(s, r)):
            if s == r and t >= first:
                te.wait_ge(sem.kq2, 1)
            blk = _block(s, t)
            kcol = (2 * s + t) * W
            for qi, top, base in ((0, r, 0), (1, NB - 1 - r, r + 1)):
                if blk > top:
                    continue
                mm, cp = sem["mm%d" % i], sem["cp%d" % i]
                bank = T.ps[:, (i % NBANKS) * BANK:(i % NBANKS) * BANK + W]
                ycol = (base + blk) * W
                if i >= NBANKS:
                    te.wait_ge(sem["cp%d" % (i - NBANKS)], 1)
                te.matmul_mx(bank, T.kc[:, kcol:kcol + W], T.ks[:, kcol:kcol + W],
                             T.qc[:, qi * W:(qi + 1) * W], T.qs[:, qi * W:(qi + 1) * W], True, True).then_inc(mm, 1)
                if i % 2 == 0:
                    v.wait_ge(mm, 1)
                    v.tensor_copy(T.yb[:, ycol:ycol + W], bank).then_inc(cp, 1)
                    q, done = sy, sem.sty
                else:
                    sc.wait_ge(mm, 1)
                    sc.activation(T.yb[:, ycol:ycol + W], bank, ActivationFunctionType.Copy).then_inc(cp, 1)
                    q, done = sc, sem.sta
                if stores[i % 2] == 0:
                    q.wait_ge(sem.fed, fed)
                q.wait_ge(cp, 1)
                q.dma_start(T.y[:, ycol:ycol + W], T.yb[:, ycol:ycol + W]).then_inc(done, 16)
                stores[i % 2] += 1
                i += 1
    sy.wait_ge(sem.sty, 16 * stores[0])
    sc.wait_ge(sem.sta, 16 * stores[1])
